import numpy as np
import ml_dtypes


def mxq(x, axis, fmt="e4m3"):
    dtype, down = {"e4m3": (ml_dtypes.float8_e4m3fn, 7), "e5m2": (ml_dtypes.float8_e5m2, 14)}[fmt]
    v = np.moveaxis(np.asarray(x, np.float32).astype(ml_dtypes.bfloat16).astype(np.float64), axis, -1)
    blocks = v.reshape(v.shape[:-1] + (-1, 32))
    amax = np.abs(blocks).max(-1, keepdims=True)
    byte = np.maximum(np.where(amax > 0, np.frexp(amax)[1] - 1 + 127, 0) - down, 1)
    scale = np.exp2(byte - 127.0)
    codes = (blocks / scale).astype(np.float32).astype(dtype).astype(np.float64)
    return np.moveaxis((codes * scale).reshape(v.shape), -1, axis)


WIDE = False


def mx_kscale(k):
    if not WIDE:
        return np.ones(k)
    levels = np.array([10, -10, 5, -5, 0])
    if k % 512:
        return np.exp2(np.random.permutation(np.resize(levels, k // 32))).repeat(32)
    a = np.empty((k // 512, 16))
    for p in range(k // 512):
        a[p, :8] = np.random.permutation(np.resize(levels, 8))
        for g in range(8):
            far = levels[np.abs(levels - a[p, g]) >= 10]
            a[p, g + 8] = far[np.random.randint(len(far))]
    return np.exp2(a.ravel()).repeat(32)


def f64(x):
    return np.asarray(x).astype(np.float64)


def striped(idx):
    return np.tile(np.asarray(idx).reshape(-1, 16).T, (8, 1)).astype(np.uint16)


def unstriped(offs):
    return offs[:16].T.reshape(-1).astype(np.int64)


E2M1 = np.array([0.0, 0.5, 1.0, 1.5, 2.0, 3.0, 4.0, 6.0, -0.0, -0.5, -1.0, -1.5, -2.0, -3.0, -4.0, -6.0])


def pack_weight(w, fmt):
    k, n = w.shape
    w = f64(np.asarray(w, np.float32).astype(ml_dtypes.bfloat16)).reshape(k // 32, 32, n)
    amax = np.abs(w).max(1)
    if fmt == "e4m3":
        byte = np.frexp(amax)[1] - 1 + 127 - 7
    else:
        mant, ex = np.frexp(amax / 6.0)
        byte = np.where(mant > 0.5, ex, ex - 1) + 127
    byte = np.clip(np.where(amax > 0, byte, 1), 1, 254)
    scaled = (w * np.exp2(127.0 - byte)[:, None, :]).reshape(k, n).astype(np.float32)
    by_word = np.ascontiguousarray(scaled.reshape(k // 512, 128, 4, n).transpose(0, 1, 3, 2))
    if fmt == "e4m3":
        words = by_word.astype(ml_dtypes.float8_e4m3fn).view(np.uint8)
    else:
        c = by_word.astype(ml_dtypes.float4_e2m1fn).view(np.uint8) & 0xF
        words = (c[..., 0::2] | (c[..., 1::2] << 4)).reshape(k // 512, 128, 2 * n)
    return np.ascontiguousarray(words), np.ascontiguousarray(byte.astype(np.uint8).reshape(k // 512, 16, n))


def unpack_weight(words, scales, fmt):
    g, _, n = scales.shape
    words = np.ascontiguousarray(words).reshape(g, 128, n, -1)
    if fmt == "e4m3":
        vals = words.view(ml_dtypes.float8_e4m3fn).astype(np.float64)
    else:
        nib = np.empty((g, 128, n, 4), np.uint8)
        nib[..., 0::2] = words & 0xF
        nib[..., 1::2] = words >> 4
        vals = E2M1[nib]
    vals = vals * np.repeat(np.exp2(scales.astype(np.float64) - 127.0), 8, axis=1)[..., None]
    return vals.transpose(0, 1, 3, 2).reshape(g * 512, n)


D, E, T, I, Q = 512, 512, 2048, 512, 128


def setup_inputs():
    n = np.random.standard_normal
    idx = np.random.permutation(T)[:I]
    fd = mx_kscale(D)
    fe = mx_kscale(E)
    fi = mx_kscale(I)
    ti = np.ones(T)
    ti[idx] = fi
    keysp = pack_weight(n((D, T)) / fd[:, None], "e4m3")
    valsp = pack_weight(n((E, T)) / fe[:, None], "e4m3")
    return {
        "query": (n((D, Q)) * 0.9 / np.sqrt(D) * fd[:, None]).astype(np.float32),
        "query2": (n((D, Q)) * 0.6 / np.sqrt(D) * fd[:, None]).astype(np.float32),
        "keys_words": keysp[0],
        "keys_scales": keysp[1],
        "gout": (n((E, Q)) * 1 / np.sqrt(E) * fe[:, None]).astype(np.float32),
        "vals_words": valsp[0],
        "vals_scales": valsp[1],
        "size": (np.random.uniform(0.5, 2.0, (1, I))).astype(np.float32),
        "dquery": (n((D, Q)) * 1.0 / np.sqrt(D) * fd[:, None]).astype(np.float32),
        "fs": (np.random.uniform(128.0, 512.0, (1, I)) * fi).astype(np.float32),
        "keyrows": (n((D, T)) / ti).astype(np.float32),
        "res": (n((Q, D)) * 4.0).astype(np.float32),
        "offs": striped(idx),
    }


def reference(query, query2, keys_words, keys_scales, gout, vals_words, vals_scales, size, dquery, fs, keyrows, res, offs):
    idx = unstriped(offs)
    keysu = unpack_weight(keys_words, keys_scales, "e4m3")
    valsu = unpack_weight(vals_words, vals_scales, "e4m3")
    queryq = mxq(f64(query), 0, "e4m3")
    keysidxg = keysu[:, idx]
    a = queryq.T @ keysidxg
    dqueryq = mxq(f64(dquery), 0, "e4m3")
    ta = dqueryq.T @ keysidxg
    query2q = mxq(f64(query2), 0, "e4m3")
    b = query2q.T @ keysidxg
    pa = np.exp(a - np.max(a, axis=1, keepdims=True))
    wa = pa / np.sum(pa, axis=1, keepdims=True)
    pb = np.exp(b - np.max(b, axis=1, keepdims=True))
    wb = pb / np.sum(pb, axis=1, keepdims=True)
    goutq = mxq(f64(gout), 0, "e4m3")
    valsidxg = valsu[:, idx]
    c0 = goutq.T @ valsidxg
    dwa = c0 * f64(size) / (wa + wb) * wb - c0 * f64(size) * wa * wb / np.square(wa + wb)
    dpa = dwa / np.sum(pa, axis=1, keepdims=True) + np.sum(dwa * pa / np.square(np.sum(pa, axis=1, keepdims=True)) * (-1.0), axis=1, keepdims=True)
    tpa = ta * pa
    twa = (tpa - np.sum(tpa, axis=1, keepdims=True) * pa / np.sum(pa, axis=1, keepdims=True)) / np.sum(pa, axis=1, keepdims=True)
    tdwa = twa * c0 * f64(size) / np.square(wa + wb) * (-1.0) * wb - (twa * wb * c0 * f64(size) - twa * (wa + wb) * 2.0 * c0 * f64(size) * wa * wb / np.square(wa + wb)) / np.square(wa + wb)
    tdpa = (tdwa - np.sum(tpa, axis=1, keepdims=True) * dwa / np.sum(pa, axis=1, keepdims=True)) / np.sum(pa, axis=1, keepdims=True) + np.sum((tdwa * pa + tpa * dwa - np.sum(tpa, axis=1, keepdims=True) * np.sum(pa, axis=1, keepdims=True) * 2.0 * dwa * pa / np.square(np.sum(pa, axis=1, keepdims=True))) / np.square(np.sum(pa, axis=1, keepdims=True)) * (-1.0), axis=1, keepdims=True)
    tda = tdpa * pa + tpa * dpa
    gs = tda * f64(fs)
    gt1 = gs.T
    kt = f64(keyrows)[:, idx].T
    gt1q = mxq(gt1, 0, "e4m3")
    ktq = mxq(kt, 0, "e4m3")
    gq = gt1q.T @ ktq
    y = gq + f64(res)
    return y

@@ -1,0 +1,269 @@
+import math
+from contextlib import ExitStack
+
+import concourse.mybir as mybir
+from concourse.masks import make_identity
+
+D, E, T, I, Q = 512, 512, 2048, 512, 128
+FLOPS = 5 * 2 * Q * I * D
+
+F32 = mybir.dt.float32
+BF16 = mybir.dt.bfloat16
+I32 = mybir.dt.int32
+U32 = mybir.dt.uint32
+U16 = mybir.dt.uint16
+U8 = mybir.dt.uint8
+FP8X4 = mybir.dt.float8_e4m3fn_x4
+ACT = mybir.ActivationFunctionType
+ALU = mybir.AluOpType
+AX = mybir.AxisListType
+
+P = 128
+PACK = 4
+VALS_PLANE = 4
+LN2 = math.log(2.0)
+LOG_PER_BIT = LN2 / 2.0**23
+LOG_OFFSET = -44.0
+
+
+def tile_attend_hvagreement_q_kernel(
+    tc, query, query2, keys_words, keys_scales, gout, vals_words, vals_scales, size, dquery, fs, keyrows, res, offs, out
+):
+    nc = tc.nc
+    with ExitStack() as ctx:
+        sb = ctx.enter_context(tc.tile_pool(name="sb", bufs=1))
+        ps = ctx.enter_context(tc.psum_pool(name="ps", bufs=1))
+        ps_turn = ctx.enter_context(tc.psum_pool(name="ps_turn", bufs=3))
+
+        def sbuf(name, shape, dtype=F32, tag=None):
+            return sb.tile(shape, dtype, name=name, tag=tag or name, align_bytes=64)
+
+        def column(name):
+            return sbuf(name, [P, 1])
+
+        def dealt(bank):
+            return bank[:].rearrange("p (s t) -> p t s", t=PACK)
+
+        offsets = sb.tile([P, I // 16], U16, name="offsets")
+        key_scale_pool = sbuf("key_scale_pool", [P, T], U8)
+        val_scale_pool = sbuf("val_scale_pool", [P, T], U8)
+        key_word_pool = sbuf("key_word_pool", [P, T], U32)
+        val_word_pool = sbuf("val_word_pool", [P, T], U32)
+        raw = [sbuf("raw%d" % n, [P, PACK, Q]) for n in range(4)]
+        key_rows = [sbuf("key_rows%d" % c, [P, T]) for c in range(4)]
+        size_by_place = sbuf("size_by_place", [P, PACK])
+        fs_by_place = sbuf("fs_by_place", [P, PACK])
+        residual = sbuf("residual", [P, D])
+        identity = sbuf("identity", [P, P])
+        warm = column("warm")
+        warm2 = column("warm2")
+
+        nc.vector.memset(key_scale_pool[:].bitcast(I32), 0)
+        nc.gpsimd.memset(val_scale_pool[:].bitcast(I32), 0)
+        nc.gpsimd.memset(warm[:], 0.0)
+        nc.scalar.activation(warm2[:], warm[:], ACT.Exp)
+        make_identity(nc, identity[:])
+
+        def load_rows(n, src):
+            nc.sync.dma_start(out=raw[n][:], in_=src.rearrange("(p j) q -> p j q", j=PACK))
+
+        def load_scales(pool, src, first):
+            for quad in range(4):
+                nc.sync.dma_start(
+                    out=pool[32 * quad + first : 32 * quad + first + 4, :].bitcast(I32),
+                    in_=src[0, 4 * quad : 4 * quad + 4, :].bitcast(I32),
+                )
+
+        def load_words(pool, src):
+            nc.sync.dma_start(out=pool[:].bitcast(I32), in_=src[0].rearrange("p n t -> p (n t)").bitcast(I32))
+
+        nc.sync.dma_start(offsets[:], offs)
+        load_rows(0, query)
+        load_scales(key_scale_pool, keys_scales, 0)
+        load_words(key_word_pool, keys_words)
+        load_rows(1, query2)
+        load_scales(val_scale_pool, vals_scales, VALS_PLANE)
+        load_rows(3, dquery)
+        load_rows(2, gout)
+        nc.sync.dma_start(out=size_by_place[:], in_=size.rearrange("o (p t) -> (o p) t", t=PACK))
+        load_words(val_word_pool, vals_words)
+        nc.sync.dma_start(out=fs_by_place[:], in_=fs.rearrange("o (p t) -> (o p) t", t=PACK))
+        for c in range(4):
+            nc.sync.dma_start(out=key_rows[c][:], in_=keyrows[c * P : (c + 1) * P, :])
+        nc.sync.dma_start(out=residual[:], in_=res)
+
+        q_codes = [sbuf("q_codes%d" % n, [P, Q], U32) for n in range(4)]
+        q_scales = [sbuf("q_scales%d" % n, [P, Q], U8) for n in range(4)]
+
+        def quantise_rows(n):
+            woven = sbuf("q_woven%d" % n, [P, Q, PACK], BF16)
+            nc.scalar.copy(woven[:], raw[n][:].rearrange("p j q -> p q j"))
+            nc.vector.quantize_mx(
+                out=q_codes[n][:].bitcast(FP8X4), scales=q_scales[n][:], in_=woven[:].rearrange("p q j -> p (q j)")
+            )
+
+        key_words = sbuf("key_words", [P, I], U32)
+        key_scales = sbuf("key_scales", [P, I], U8)
+        val_words = sbuf("val_words", [P, I], U32)
+        val_scales = sbuf("val_scales", [P, I], U8)
+
+        def gather(dst, pool):
+            nc.vector.tensor_copy(dst[:], pool[:].indirect(offsets[:]))
+
+        def score(bank, n):
+            nc.tensor.matmul_mx(
+                out=bank[:], lhsT=q_codes[n][:].bitcast(FP8X4), lhsT_scale=q_scales[n][:],
+                rhs=key_words[:].bitcast(FP8X4), rhs_scale=key_scales[:], start=True, stop=True,
+            )
+
+        gather(key_scales, key_scale_pool)
+        quantise_rows(0)
+        gather(key_words, key_word_pool)
+        quantise_rows(1)
+        a = ps.tile([P, I], F32, name="a", tag="bank_a")
+        b = ps.tile([P, I], F32, name="b", tag="bank_b")
+        ta = ps.tile([P, I], F32, name="ta", tag="bank_ta")
+        score(a, 0)
+        score(b, 1)
+        gather(val_scales, val_scale_pool)
+        quantise_rows(3)
+        quantise_rows(2)
+
+        neg_a = sbuf("neg_a", [P, PACK, P])
+        neg_max_a = column("neg_max_a")
+        neg_max_b = column("neg_max_b")
+        nc.vector.tensor_scalar(neg_a[:], dealt(a), -1.0, None, ALU.mult, ALU.min, accum_out=neg_max_a[:])
+        nc.vector.tensor_reduce(neg_max_b[:], b[:], AX.X, ALU.max, negate=True)
+
+        pa = sbuf("pa", [P, PACK, P], tag="raw2")
+        pb = sbuf("pb", [P, I], BF16)
+        sum_a = sbuf("sum_a", [P, 1], tag="raw3")
+        sum_b = column("sum_b")
+        nc.scalar.activation(pa[:], dealt(a), ACT.Exp, bias=neg_max_a[:], accum_out=sum_a[:])
+        nc.scalar.activation(pb[:], b[:], ACT.Exp, bias=neg_max_b[:], accum_out=sum_b[:])
+
+        max_gap = column("max_gap")
+        inv_a = column("inv_a")
+        neg_inv_a = column("neg_inv_a")
+        gap = sbuf("gap", [P, PACK, P])
+        nc.vector.tensor_tensor(max_gap[:], neg_max_b[:], neg_max_a[:], ALU.subtract)
+        nc.vector.reciprocal(inv_a[:], sum_a[:])
+        nc.vector.scalar_tensor_tensor(gap[:], dealt(b), max_gap[:], neg_a[:], ALU.add, ALU.add)
+
+        e0 = column("e0")
+        v0 = column("v0")
+        sq = column("sq")
+        v1 = column("v1")
+        e1 = column("e1")
+        half_log = column("half_log")
+        ratio = column("ratio")
+        sq1 = column("sq1")
+        nc.scalar.activation(ratio[:], sum_b[:], ACT.Copy, scale=inv_a[:])
+        bits = ratio[:].bitcast(U32)
+        nc.scalar.activation(e0[:], bits, ACT.Exp, scale=-LOG_PER_BIT, bias=-2.0 * LOG_OFFSET)
+        nc.scalar.activation(v0[:], bits, ACT.Identity, scale=0.5 * LOG_PER_BIT, bias=LOG_OFFSET + 0.5)
+        nc.scalar.activation(sq[:], e0[:], ACT.Square, scale=ratio[:], bias=-2.0)
+        nc.scalar.activation(v1[:], sq[:], ACT.Identity, scale=-0.25, bias=v0[:])
+        nc.scalar.activation(e1[:], v1[:], ACT.Exp, scale=-2.0, bias=0.5)
+        nc.scalar.activation(sq1[:], e1[:], ACT.Square, scale=ratio[:], bias=-2.0)
+        nc.scalar.activation(half_log[:], sq1[:], ACT.Identity, scale=-0.25, bias=v1[:])
+        nc.scalar.activation(neg_inv_a[:], inv_a[:], ACT.Copy, scale=-1.0)
+        tilt = sbuf("tilt", [P, PACK, P])
+        share_sq = sbuf("share_sq", [P, PACK, P])
+        nc.scalar.activation(tilt[:], gap[:], ACT.Tanh, scale=-0.5, bias=half_log[:])
+        nc.scalar.activation(share_sq[:], tilt[:], ACT.Square, scale=-0.5, bias=0.5)
+
+        gather(val_words, val_word_pool)
+        score(ta, 3)
+        size_spread = ps.tile([P, PACK, P], F32, name="size_spread", tag="bank_size")
+        for t in range(PACK):
+            nc.tensor.transpose(size_spread[:, t, :], size_by_place[:, t : t + 1].to_broadcast([P, P]), identity[:])
+        c0 = ps.tile([P, I], F32, name="c0", tag="bank_c")
+        nc.tensor.matmul_mx(
+            out=c0[:], lhsT=q_codes[2][:].bitcast(FP8X4), lhsT_scale=q_scales[2][:],
+            rhs=val_words[:].bitcast(FP8X4), rhs_scale=val_scales[VALS_PLANE:P, :], start=True, stop=True,
+        )
+        sized_pa = sbuf("sized_pa", [P, PACK, P])
+        nc.vector.tensor_tensor(sized_pa[:], size_spread[:], pa[:], ALU.mult)
+
+        tpa = sbuf("tpa", [P, PACK, P], tag="val_word_pool")
+        sum_tpa = column("sum_tpa")
+        neg_mean = column("neg_mean")
+        nc.vector.scalar_tensor_tensor(tpa[:], dealt(ta), 1.0, pa[:], ALU.mult, ALU.mult, accum_out=sum_tpa[:])
+        nc.scalar.activation(neg_mean[:], sum_tpa[:], ACT.Copy, scale=neg_inv_a[:])
+        pc = sbuf("pc", [P, PACK, P])
+        nc.vector.scalar_tensor_tensor(pc[:], dealt(c0), neg_inv_a[:], sized_pa[:], ALU.mult, ALU.mult)
+        picked = []
+
+        def pick(c, tag):
+            picked.append(sbuf("picked%d" % c, [P, I], BF16, tag=tag))
+            nc.vector.tensor_copy(picked[c][:], key_rows[c][:].indirect(offsets[:]))
+
+        pick(0, "sized_pa")
+        ut = sbuf("ut", [P, PACK, P], tag="key_rows0")
+        nc.vector.scalar_tensor_tensor(ut[:], dealt(ta), neg_mean[:], tilt[:], ALU.add, ALU.mult)
+        y = sbuf("y", [P, PACK, P])
+        neg_g = column("neg_g")
+        nc.vector.scalar_tensor_tensor(y[:], pc[:], 1.0, share_sq[:], ALU.mult, ALU.mult, accum_out=neg_g[:])
+        z = sbuf("z", [P, PACK, P])
+        sum_z = column("sum_z")
+        nc.vector.scalar_tensor_tensor(z[:], y[:], 1.0, ut[:], ALU.mult, ALU.mult, accum_out=sum_z[:])
+
+        pick(1, "key_rows0")
+        pick(2, "y")
+        pick(3, "tilt")
+        alpha = column("alpha")
+        gamma = column("gamma")
+        beta = column("beta")
+        term_tpa = sbuf("term_tpa", [P, PACK, P])
+        term_pa = sbuf("term_pa", [P, PACK, P])
+        nc.scalar.activation(alpha[:], neg_g[:], ACT.Copy, scale=inv_a[:])
+        nc.scalar.activation(gamma[:], alpha[:], ACT.Copy, scale=neg_mean[:])
+        nc.scalar.activation(term_tpa[:], tpa[:], ACT.Copy, scale=alpha[:])
+        nc.scalar.activation(beta[:], sum_z[:], ACT.Identity, scale=neg_inv_a[:], bias=gamma[:])
+        nc.scalar.activation(term_pa[:], pa[:], ACT.Copy, scale=beta[:])
+
+        tda_turned = ps.tile([P, PACK, Q], F32, name="tda_turned", tag="bank_a")
+        terms = [z, term_tpa, term_pa]
+        for n, term in enumerate(terms):
+            for t in range(PACK):
+                nc.tensor.matmul(
+                    tda_turned[:, t, :], lhsT=term[:, t, :], rhs=identity[:], is_transpose=True,
+                    start=(n == 0 and t == 0), stop=(n == len(terms) - 1 and t == PACK - 1),
+                )
+        g_woven = sbuf("g_woven", [P, Q, PACK], BF16, tag="key_rows3")
+        g_codes = sbuf("g_codes", [P, Q], U32)
+        g_scales = sbuf("g_scales", [P, Q], U8)
+        nc.vector.tensor_tensor(
+            g_woven[:], tda_turned[:].rearrange("p t q -> p q t"),
+            fs_by_place[:].unsqueeze(1).to_broadcast([P, Q, PACK]), ALU.mult,
+        )
+        nc.vector.quantize_mx(
+            out=g_codes[:].bitcast(FP8X4), scales=g_scales[:], in_=g_woven[:].rearrange("p q t -> p (q t)")
+        )
+
+        for half, tag in enumerate(("bank_b", "bank_c")):
+            kt_woven = sbuf("kt_woven%d" % half, [P, 2, P * PACK], BF16)
+            kt_codes = sbuf("kt_codes%d" % half, [P, 2 * P], U32)
+            kt_scales = sbuf("kt_scales%d" % half, [P, 2 * P], U8)
+            for n in range(2):
+                c = 2 * half + n
+                pairs = picked[c][:].bitcast(F32)
+                turned = ps_turn.tile([P, 2, P], F32, name="turned", tag="turn")
+                for u in range(2):
+                    nc.tensor.transpose(turned[:, u, :], pairs[:, u : I // 2 : 2], identity[:])
+                nc.scalar.copy(
+                    kt_woven[:, n, :].bitcast(F32).rearrange("p (d u) -> p d u", u=2), turned[:].rearrange("p u d -> p d u")
+                )
+            nc.vector.quantize_mx(
+                out=kt_codes[:].bitcast(FP8X4), scales=kt_scales[:], in_=kt_woven[:].rearrange("p n w -> p (n w)")
+            )
+            cols = slice(half * 2 * P, (half + 1) * 2 * P)
+            gq = ps.tile([P, 2 * P], F32, name="gq%d" % half, tag=tag)
+            nc.tensor.matmul_mx(
+                out=gq[:], lhsT=g_codes[:].bitcast(FP8X4), lhsT_scale=g_scales[:],
+                rhs=kt_codes[:].bitcast(FP8X4), rhs_scale=kt_scales[:], start=True, stop=True,
+            )
+            result = sbuf("result%d" % half, [P, 2 * P])
+            nc.vector.tensor_tensor(result[:], gq[:], residual[:, cols], ALU.add)
+            nc.sync.dma_start(out=out[:, cols], in_=result[:])

@@ -16,7 +16,6 @@ U8 = mybir.dt.uint8
 FP8X4 = mybir.dt.float8_e4m3fn_x4
 ACT = mybir.ActivationFunctionType
 ALU = mybir.AluOpType
-AX = mybir.AxisListType
 
 P = 128
 PACK = 4
@@ -51,7 +50,7 @@ def tile_attend_hvagreement_q_kernel(
         val_word_pool = sbuf("val_word_pool", [P, T], U32)
         raw = [sbuf("raw%d" % n, [P, PACK, Q]) for n in range(4)]
         key_rows = [sbuf("key_rows%d" % c, [P, T]) for c in range(4)]
-        size_by_place = sbuf("size_by_place", [P, PACK])
+        size_rows = sbuf("size_rows", [P, P])
         fs_by_place = sbuf("fs_by_place", [P, PACK])
         residual = sbuf("residual", [P, D])
         identity = sbuf("identity", [P, P])
@@ -61,6 +60,8 @@ def tile_attend_hvagreement_q_kernel(
         nc.vector.memset(key_scale_pool[:].bitcast(I32), 0)
         nc.gpsimd.memset(val_scale_pool[:].bitcast(I32), 0)
         nc.gpsimd.memset(warm[:], 0.0)
+        nc.gpsimd.memset(size_rows[:], 0.0)
+        nc.gpsimd.dma_start(out=size_rows[0:4, :], in_=size.rearrange("o (r c) -> (o r) c", r=4))
         nc.scalar.activation(warm2[:], warm[:], ACT.Exp)
         make_identity(nc, identity[:])
 
@@ -85,15 +86,14 @@ def tile_attend_hvagreement_q_kernel(
         load_scales(val_scale_pool, vals_scales, VALS_PLANE)
         load_rows(3, dquery)
         load_rows(2, gout)
-        nc.sync.dma_start(out=size_by_place[:], in_=size.rearrange("o (p t) -> (o p) t", t=PACK))
         load_words(val_word_pool, vals_words)
         nc.sync.dma_start(out=fs_by_place[:], in_=fs.rearrange("o (p t) -> (o p) t", t=PACK))
         for c in range(4):
             nc.sync.dma_start(out=key_rows[c][:], in_=keyrows[c * P : (c + 1) * P, :])
         nc.sync.dma_start(out=residual[:], in_=res)
 
-        q_codes = [sbuf("q_codes%d" % n, [P, Q], U32) for n in range(4)]
-        q_scales = [sbuf("q_scales%d" % n, [P, Q], U8) for n in range(4)]
+        q_codes = [sbuf("q_codes%d" % n, [P, Q], U32) for n in range(2)]
+        q_scales = [sbuf("q_scales%d" % n, [P, Q], U8) for n in range(2)]
 
         def quantise_rows(n):
             woven = sbuf("q_woven%d" % n, [P, Q, PACK], BF16)
@@ -126,14 +126,18 @@ def tile_attend_hvagreement_q_kernel(
         score(a, 0)
         score(b, 1)
         gather(val_scales, val_scale_pool)
-        quantise_rows(3)
-        quantise_rows(2)
+        late_woven = sbuf("late_woven", [P, 2, Q, PACK], BF16)
+        late_codes = sbuf("late_codes", [P, 2, Q], U32)
+        late_scales = sbuf("late_scales", [P, 2, Q], U8)
+        for n in range(2):
+            nc.scalar.copy(late_woven[:, n, :, :], raw[3 - n][:].rearrange("p j q -> p q j"))
 
         neg_a = sbuf("neg_a", [P, PACK, P])
         neg_max_a = column("neg_max_a")
         neg_max_b = column("neg_max_b")
         nc.vector.tensor_scalar(neg_a[:], dealt(a), -1.0, None, ALU.mult, ALU.min, accum_out=neg_max_a[:])
-        nc.vector.tensor_reduce(neg_max_b[:], b[:], AX.X, ALU.max, negate=True)
+        neg_b = sbuf("neg_b", [P, PACK, P])
+        nc.vector.tensor_scalar(neg_b[:], dealt(b), -1.0, None, ALU.mult, ALU.min, accum_out=neg_max_b[:])
 
         pa = sbuf("pa", [P, PACK, P], tag="raw2")
         pb = sbuf("pb", [P, I], BF16)
@@ -147,8 +151,13 @@ def tile_attend_hvagreement_q_kernel(
         neg_inv_a = column("neg_inv_a")
         gap = sbuf("gap", [P, PACK, P])
         nc.vector.tensor_tensor(max_gap[:], neg_max_b[:], neg_max_a[:], ALU.subtract)
+        nc.vector.scalar_tensor_tensor(gap[:], neg_a[:], max_gap[:], neg_b[:], ALU.add, ALU.subtract)
         nc.vector.reciprocal(inv_a[:], sum_a[:])
-        nc.vector.scalar_tensor_tensor(gap[:], dealt(b), max_gap[:], neg_a[:], ALU.add, ALU.add)
+        nc.vector.quantize_mx(
+            out=late_codes[:].rearrange("p n q -> p (n q)").bitcast(FP8X4),
+            scales=late_scales[:].rearrange("p n q -> p (n q)"),
+            in_=late_woven[:].rearrange("p n q j -> p (n q j)"),
+        )
 
         e0 = column("e0")
         v0 = column("v0")
@@ -171,37 +180,48 @@ def tile_attend_hvagreement_q_kernel(
         tilt = sbuf("tilt", [P, PACK, P])
         share_sq = sbuf("share_sq", [P, PACK, P])
         nc.scalar.activation(tilt[:], gap[:], ACT.Tanh, scale=-0.5, bias=half_log[:])
-        nc.scalar.activation(share_sq[:], tilt[:], ACT.Square, scale=-0.5, bias=0.5)
 
         gather(val_words, val_word_pool)
-        score(ta, 3)
-        size_spread = ps.tile([P, PACK, P], F32, name="size_spread", tag="bank_size")
-        for t in range(PACK):
-            nc.tensor.transpose(size_spread[:, t, :], size_by_place[:, t : t + 1].to_broadcast([P, P]), identity[:])
-        c0 = ps.tile([P, I], F32, name="c0", tag="bank_c")
         nc.tensor.matmul_mx(
-            out=c0[:], lhsT=q_codes[2][:].bitcast(FP8X4), lhsT_scale=q_scales[2][:],
-            rhs=val_words[:].bitcast(FP8X4), rhs_scale=val_scales[VALS_PLANE:P, :], start=True, stop=True,
+            out=ta[:], lhsT=late_codes[:, 0, :].bitcast(FP8X4), lhsT_scale=late_scales[:, 0, :],
+            rhs=key_words[:].bitcast(FP8X4), rhs_scale=key_scales[:], start=True, stop=True,
         )
-        sized_pa = sbuf("sized_pa", [P, PACK, P])
-        nc.vector.tensor_tensor(sized_pa[:], size_spread[:], pa[:], ALU.mult)
+        size_turned = ps_turn.tile([P, P], F32, name="size_turned", tag="turn")
+        size_cols = sbuf("size_cols", [P, 4])
+        nc.tensor.transpose(size_turned[:], size_rows[:], identity[:])
+        nc.scalar.copy(size_cols[:], size_turned[:, 0:4])
+        c0_by_slot = ps.tile([P, 4, Q], F32, name="c0_by_slot", tag="bank_c")
+        cs_by_slot = sbuf("cs_by_slot", [P, 4, Q], tag="gap")
+        cs = ps.tile([P, I], F32, name="cs", tag="bank_cs")
+        for r in range(4):
+            cols = slice(r * P, (r + 1) * P)
+            nc.tensor.matmul_mx(
+                out=c0_by_slot[:, r, :], lhsT=val_words[:, cols].bitcast(FP8X4), lhsT_scale=val_scales[VALS_PLANE:P, cols],
+                rhs=late_codes[:, 1, :].bitcast(FP8X4), rhs_scale=late_scales[:, 1, :], start=True, stop=True,
+            )
+        for r in range(4):
+            nc.scalar.activation(cs_by_slot[:, r, :], c0_by_slot[:, r, :], ACT.Copy, scale=size_cols[:, r : r + 1])
+        nc.scalar.activation(share_sq[:], tilt[:], ACT.Square, scale=-0.5, bias=0.5)
+        for r in range(4):
+            nc.tensor.transpose(cs[:, r * P : (r + 1) * P], cs_by_slot[:, r, :], identity[:])
 
         tpa = sbuf("tpa", [P, PACK, P], tag="val_word_pool")
         sum_tpa = column("sum_tpa")
         neg_mean = column("neg_mean")
         nc.vector.scalar_tensor_tensor(tpa[:], dealt(ta), 1.0, pa[:], ALU.mult, ALU.mult, accum_out=sum_tpa[:])
         nc.scalar.activation(neg_mean[:], sum_tpa[:], ACT.Copy, scale=neg_inv_a[:])
-        pc = sbuf("pc", [P, PACK, P])
-        nc.vector.scalar_tensor_tensor(pc[:], dealt(c0), neg_inv_a[:], sized_pa[:], ALU.mult, ALU.mult)
         picked = []
 
-        def pick(c, tag):
-            picked.append(sbuf("picked%d" % c, [P, I], BF16, tag=tag))
+        def pick(c):
+            picked.append(sbuf("picked%d" % c, [P, I], BF16))
             nc.vector.tensor_copy(picked[c][:], key_rows[c][:].indirect(offsets[:]))
 
-        pick(0, "sized_pa")
-        ut = sbuf("ut", [P, PACK, P], tag="key_rows0")
+        pick(0)
+        pick(1)
+        ut = sbuf("ut", [P, PACK, P], tag="key_rows1")
         nc.vector.scalar_tensor_tensor(ut[:], dealt(ta), neg_mean[:], tilt[:], ALU.add, ALU.mult)
+        pc = sbuf("pc", [P, PACK, P], tag="key_rows0")
+        nc.vector.scalar_tensor_tensor(pc[:], dealt(cs), neg_inv_a[:], pa[:], ALU.mult, ALU.mult)
         y = sbuf("y", [P, PACK, P])
         neg_g = column("neg_g")
         nc.vector.scalar_tensor_tensor(y[:], pc[:], 1.0, share_sq[:], ALU.mult, ALU.mult, accum_out=neg_g[:])
@@ -209,9 +229,8 @@ def tile_attend_hvagreement_q_kernel(
         sum_z = column("sum_z")
         nc.vector.scalar_tensor_tensor(z[:], y[:], 1.0, ut[:], ALU.mult, ALU.mult, accum_out=sum_z[:])
 
-        pick(1, "key_rows0")
-        pick(2, "y")
-        pick(3, "tilt")
+        pick(2)
+        pick(3)
         alpha = column("alpha")
         gamma = column("gamma")
         beta = column("beta")
@@ -248,10 +267,11 @@ def tile_attend_hvagreement_q_kernel(
             kt_scales = sbuf("kt_scales%d" % half, [P, 2 * P], U8)
             for n in range(2):
                 c = 2 * half + n
-                pairs = picked[c][:].bitcast(F32)
+                pairs = sbuf("pairs%d" % c, [P, 2, P])
+                nc.scalar.copy(pairs[:], picked[c][:].bitcast(F32).rearrange("p (s u) -> p u s", u=2))
                 turned = ps_turn.tile([P, 2, P], F32, name="turned", tag="turn")
                 for u in range(2):
-                    nc.tensor.transpose(turned[:, u, :], pairs[:, u : I // 2 : 2], identity[:])
+                    nc.tensor.transpose(turned[:, u, :], pairs[:, u, :], identity[:])
                 nc.scalar.copy(
                     kt_woven[:, n, :].bitcast(F32).rearrange("p (d u) -> p d u", u=2), turned[:].rearrange("p u d -> p d u")
                 )

@@ -4,7 +4,7 @@ from contextlib import ExitStack
 import concourse.mybir as mybir
 from concourse.masks import make_identity
 
-D, E, T, I, Q = 512, 512, 2048, 512, 128
+D, T, I, Q = 512, 2048, 512, 128
 FLOPS = 5 * 2 * Q * I * D
 
 F32 = mybir.dt.float32
@@ -18,11 +18,12 @@ ACT = mybir.ActivationFunctionType
 ALU = mybir.AluOpType
 
 P = 128
-PACK = 4
-VALS_PLANE = 4
-LN2 = math.log(2.0)
-LOG_PER_BIT = LN2 / 2.0**23
-LOG_OFFSET = -44.0
+PLACES = 4
+RUN = 8
+QUADRANT = 32
+VAL_PLANE_ROW = 4
+LOG_PER_BIT = math.log(2.0) / 2.0**23
+HALF_LOG_OFFSET = -44.0
 
 
 def tile_attend_hvagreement_q_kernel(
@@ -34,256 +35,259 @@ def tile_attend_hvagreement_q_kernel(
         ps = ctx.enter_context(tc.psum_pool(name="ps", bufs=1))
         ps_turn = ctx.enter_context(tc.psum_pool(name="ps_turn", bufs=3))
 
-        def sbuf(name, shape, dtype=F32, tag=None):
-            return sb.tile(shape, dtype, name=name, tag=tag or name, align_bytes=64)
+        def sbuf(name, shape, dtype=F32, after=None):
+            return sb.tile(shape, dtype, name=name, tag=after or name, align_bytes=64)
 
-        def column(name):
-            return sbuf(name, [P, 1])
+        def column(name, after=None):
+            return sbuf(name, [P, 1], after=after)
 
-        def dealt(bank):
-            return bank[:].rearrange("p (s t) -> p t s", t=PACK)
+        def list_order(dealt_tile, run=RUN):
+            return dealt_tile.rearrange("p (t g j) -> p g t j", t=PLACES, j=run)
+
+        def dealt_order(listed_tile, run=RUN):
+            return listed_tile.rearrange("p (g t j) -> p t g j", t=PLACES, j=run)
+
+        def by_place(tile, run=RUN):
+            return tile.rearrange("p (t g j) -> p t g j", t=PLACES, j=run)
+
+        def product(bank, left_codes, left_scales, right_codes, right_scales):
+            nc.tensor.matmul_mx(
+                out=bank, lhsT=left_codes.bitcast(FP8X4), lhsT_scale=left_scales,
+                rhs=right_codes.bitcast(FP8X4), rhs_scale=right_scales, start=True, stop=True,
+            )
+
+        def quantise(codes, scales, woven):
+            nc.vector.quantize_mx(out=codes.bitcast(FP8X4), scales=scales, in_=woven)
 
         offsets = sb.tile([P, I // 16], U16, name="offsets")
         key_scale_pool = sbuf("key_scale_pool", [P, T], U8)
         val_scale_pool = sbuf("val_scale_pool", [P, T], U8)
         key_word_pool = sbuf("key_word_pool", [P, T], U32)
         val_word_pool = sbuf("val_word_pool", [P, T], U32)
-        raw = [sbuf("raw%d" % n, [P, PACK, Q]) for n in range(4)]
-        key_rows = [sbuf("key_rows%d" % c, [P, T]) for c in range(4)]
-        size_rows = sbuf("size_rows", [P, P])
-        fs_by_place = sbuf("fs_by_place", [P, PACK])
+        query_raw = sbuf("query_raw", [P, PLACES, Q])
+        query2_raw = sbuf("query2_raw", [P, PLACES, Q])
+        dquery_raw = sbuf("dquery_raw", [P, PLACES, Q])
+        gout_raw = sbuf("gout_raw", [P, PLACES, Q])
+        key_rows = [sbuf("key_rows%d" % c, [P, T]) for c in range(D // P)]
+        slot_rows = sbuf("slot_rows", [P, P])
         residual = sbuf("residual", [P, D])
         identity = sbuf("identity", [P, P])
-        warm = column("warm")
-        warm2 = column("warm2")
+        identity_bf = sbuf("identity_bf", [P, P], BF16)
+        zero = column("zero")
+        table_warm = column("table_warm")
 
         nc.vector.memset(key_scale_pool[:].bitcast(I32), 0)
         nc.gpsimd.memset(val_scale_pool[:].bitcast(I32), 0)
-        nc.gpsimd.memset(warm[:], 0.0)
-        nc.gpsimd.memset(size_rows[:], 0.0)
-        nc.gpsimd.dma_start(out=size_rows[0:4, :], in_=size.rearrange("o (r c) -> (o r) c", r=4))
-        nc.scalar.activation(warm2[:], warm[:], ACT.Exp)
+        nc.gpsimd.memset(zero[:], 0.0)
+        nc.scalar.activation(table_warm[:], zero[:], ACT.Exp)
+        nc.gpsimd.memset(slot_rows[:], 0.0)
+        nc.gpsimd.dma_start(out=slot_rows[0:PLACES, :], in_=size.rearrange("o (r c) -> (o r) c", r=PLACES))
+        nc.gpsimd.dma_start(
+            out=slot_rows[PLACES : 2 * PLACES, :].rearrange("t (g j) -> t g j", j=RUN),
+            in_=fs.rearrange("o (g t j) -> (o t) g j", t=PLACES, j=RUN),
+        )
         make_identity(nc, identity[:])
+        make_identity(nc, identity_bf[:])
 
-        def load_rows(n, src):
-            nc.sync.dma_start(out=raw[n][:], in_=src.rearrange("(p j) q -> p j q", j=PACK))
+        def load_rows(raw, src):
+            nc.sync.dma_start(out=raw[:], in_=src.rearrange("(p t) q -> p t q", t=PLACES))
 
-        def load_scales(pool, src, first):
-            for quad in range(4):
-                nc.sync.dma_start(
-                    out=pool[32 * quad + first : 32 * quad + first + 4, :].bitcast(I32),
-                    in_=src[0, 4 * quad : 4 * quad + 4, :].bitcast(I32),
-                )
+        def load_scales(pool, src, first_row):
+            for quad in range(P // QUADRANT):
+                row = QUADRANT * quad + first_row
+                nc.sync.dma_start(out=pool[row : row + 4, :].bitcast(I32), in_=src[0, 4 * quad : 4 * quad + 4, :].bitcast(I32))
 
         def load_words(pool, src):
             nc.sync.dma_start(out=pool[:].bitcast(I32), in_=src[0].rearrange("p n t -> p (n t)").bitcast(I32))
 
         nc.sync.dma_start(offsets[:], offs)
-        load_rows(0, query)
+        load_rows(query_raw, query)
         load_scales(key_scale_pool, keys_scales, 0)
         load_words(key_word_pool, keys_words)
-        load_rows(1, query2)
-        load_scales(val_scale_pool, vals_scales, VALS_PLANE)
-        load_rows(3, dquery)
-        load_rows(2, gout)
+        load_rows(query2_raw, query2)
+        load_scales(val_scale_pool, vals_scales, VAL_PLANE_ROW)
+        load_rows(dquery_raw, dquery)
+        load_rows(gout_raw, gout)
         load_words(val_word_pool, vals_words)
-        nc.sync.dma_start(out=fs_by_place[:], in_=fs.rearrange("o (p t) -> (o p) t", t=PACK))
-        for c in range(4):
+        for c in range(D // P):
             nc.sync.dma_start(out=key_rows[c][:], in_=keyrows[c * P : (c + 1) * P, :])
         nc.sync.dma_start(out=residual[:], in_=res)
 
-        q_codes = [sbuf("q_codes%d" % n, [P, Q], U32) for n in range(2)]
-        q_scales = [sbuf("q_scales%d" % n, [P, Q], U8) for n in range(2)]
-
-        def quantise_rows(n):
-            woven = sbuf("q_woven%d" % n, [P, Q, PACK], BF16)
-            nc.scalar.copy(woven[:], raw[n][:].rearrange("p j q -> p q j"))
-            nc.vector.quantize_mx(
-                out=q_codes[n][:].bitcast(FP8X4), scales=q_scales[n][:], in_=woven[:].rearrange("p q j -> p (q j)")
-            )
-
-        key_words = sbuf("key_words", [P, I], U32)
-        key_scales = sbuf("key_scales", [P, I], U8)
-        val_words = sbuf("val_words", [P, I], U32)
-        val_scales = sbuf("val_scales", [P, I], U8)
-
         def gather(dst, pool):
-            nc.vector.tensor_copy(dst[:], pool[:].indirect(offsets[:]))
+            nc.vector.tensor_copy(dst, pool[:].indirect(offsets[:]))
 
-        def score(bank, n):
-            nc.tensor.matmul_mx(
-                out=bank[:], lhsT=q_codes[n][:].bitcast(FP8X4), lhsT_scale=q_scales[n][:],
-                rhs=key_words[:].bitcast(FP8X4), rhs_scale=key_scales[:], start=True, stop=True,
-            )
+        def weave(woven, raw):
+            nc.scalar.copy(woven, raw[:].rearrange("p t q -> p q t"))
 
-        gather(key_scales, key_scale_pool)
-        quantise_rows(0)
-        gather(key_words, key_word_pool)
-        quantise_rows(1)
+        def quantise_rows(name, raw):
+            woven = sbuf(name + "_woven", [P, Q, PLACES], BF16)
+            codes = sbuf(name + "_codes", [P, Q], U32)
+            scales = sbuf(name + "_scales", [P, Q], U8)
+            weave(woven[:], raw)
+            quantise(codes[:], scales[:], woven[:].rearrange("p q t -> p (q t)"))
+            return codes, scales
+
+        listed_key_scales = sbuf("listed_key_scales", [P, I], U8)
+        key_scales = sbuf("key_scales", [P, I], U8)
+        key_words = sbuf("key_words", [P, I], U32)
+        val_scales = sbuf("val_scales", [P, I], U8)
+        val_words = sbuf("val_words", [P, I], U32)
+        gather(listed_key_scales[:], key_scale_pool)
+        query_codes, query_scales = quantise_rows("query", query_raw)
+        nc.vector.tensor_copy(
+            by_place(key_scales[:].bitcast(I32), RUN // 4), dealt_order(listed_key_scales[:].bitcast(I32), RUN // 4)
+        )
+        gather(list_order(key_words[:]), key_word_pool)
+        query2_codes, query2_scales = quantise_rows("query2", query2_raw)
         a = ps.tile([P, I], F32, name="a", tag="bank_a")
         b = ps.tile([P, I], F32, name="b", tag="bank_b")
-        ta = ps.tile([P, I], F32, name="ta", tag="bank_ta")
-        score(a, 0)
-        score(b, 1)
-        gather(val_scales, val_scale_pool)
-        late_woven = sbuf("late_woven", [P, 2, Q, PACK], BF16)
+        product(a[:], query_codes[:], query_scales[:], key_words[:], key_scales[:])
+        product(b[:], query2_codes[:], query2_scales[:], key_words[:], key_scales[:])
+        gather(val_scales[:], val_scale_pool)
+        late_woven = sbuf("late_woven", [P, 2, Q, PLACES], BF16)
         late_codes = sbuf("late_codes", [P, 2, Q], U32)
         late_scales = sbuf("late_scales", [P, 2, Q], U8)
-        for n in range(2):
-            nc.scalar.copy(late_woven[:, n, :, :], raw[3 - n][:].rearrange("p j q -> p q j"))
+        weave(late_woven[:, 0, :, :], dquery_raw)
+        weave(late_woven[:, 1, :, :], gout_raw)
 
-        neg_a = sbuf("neg_a", [P, PACK, P])
+        neg_a = sbuf("neg_a", [P, I])
+        neg_b = sbuf("neg_b", [P, I])
         neg_max_a = column("neg_max_a")
         neg_max_b = column("neg_max_b")
-        nc.vector.tensor_scalar(neg_a[:], dealt(a), -1.0, None, ALU.mult, ALU.min, accum_out=neg_max_a[:])
-        neg_b = sbuf("neg_b", [P, PACK, P])
-        nc.vector.tensor_scalar(neg_b[:], dealt(b), -1.0, None, ALU.mult, ALU.min, accum_out=neg_max_b[:])
-
-        pa = sbuf("pa", [P, PACK, P], tag="raw2")
+        nc.vector.tensor_scalar(neg_a[:], a[:], -1.0, None, ALU.mult, ALU.min, accum_out=neg_max_a[:])
+        nc.vector.tensor_scalar(neg_b[:], b[:], -1.0, None, ALU.mult, ALU.min, accum_out=neg_max_b[:])
+        pa = sbuf("pa", [P, I], after="gout_raw")
+        sum_a = column("sum_a", after="dquery_raw")
         pb = sbuf("pb", [P, I], BF16)
-        sum_a = sbuf("sum_a", [P, 1], tag="raw3")
         sum_b = column("sum_b")
-        nc.scalar.activation(pa[:], dealt(a), ACT.Exp, bias=neg_max_a[:], accum_out=sum_a[:])
+        nc.scalar.activation(pa[:], a[:], ACT.Exp, bias=neg_max_a[:], accum_out=sum_a[:])
         nc.scalar.activation(pb[:], b[:], ACT.Exp, bias=neg_max_b[:], accum_out=sum_b[:])
-
         max_gap = column("max_gap")
+        gap = sbuf("gap", [P, I])
         inv_a = column("inv_a")
-        neg_inv_a = column("neg_inv_a")
-        gap = sbuf("gap", [P, PACK, P])
         nc.vector.tensor_tensor(max_gap[:], neg_max_b[:], neg_max_a[:], ALU.subtract)
         nc.vector.scalar_tensor_tensor(gap[:], neg_a[:], max_gap[:], neg_b[:], ALU.add, ALU.subtract)
         nc.vector.reciprocal(inv_a[:], sum_a[:])
-        nc.vector.quantize_mx(
-            out=late_codes[:].rearrange("p n q -> p (n q)").bitcast(FP8X4),
-            scales=late_scales[:].rearrange("p n q -> p (n q)"),
-            in_=late_woven[:].rearrange("p n q j -> p (n q j)"),
+        quantise(
+            late_codes[:].rearrange("p n q -> p (n q)"),
+            late_scales[:].rearrange("p n q -> p (n q)"),
+            late_woven[:].rearrange("p n q t -> p (n q t)"),
         )
 
-        e0 = column("e0")
-        v0 = column("v0")
-        sq = column("sq")
-        v1 = column("v1")
-        e1 = column("e1")
-        half_log = column("half_log")
         ratio = column("ratio")
-        sq1 = column("sq1")
+        exp_guess = column("exp_guess")
+        guess = column("guess")
+        square1 = column("square1")
+        step1 = column("step1")
+        exp_step1 = column("exp_step1")
+        square2 = column("square2")
+        half_log = column("half_log")
+        neg_inv_a = column("neg_inv_a")
         nc.scalar.activation(ratio[:], sum_b[:], ACT.Copy, scale=inv_a[:])
         bits = ratio[:].bitcast(U32)
-        nc.scalar.activation(e0[:], bits, ACT.Exp, scale=-LOG_PER_BIT, bias=-2.0 * LOG_OFFSET)
-        nc.scalar.activation(v0[:], bits, ACT.Identity, scale=0.5 * LOG_PER_BIT, bias=LOG_OFFSET + 0.5)
-        nc.scalar.activation(sq[:], e0[:], ACT.Square, scale=ratio[:], bias=-2.0)
-        nc.scalar.activation(v1[:], sq[:], ACT.Identity, scale=-0.25, bias=v0[:])
-        nc.scalar.activation(e1[:], v1[:], ACT.Exp, scale=-2.0, bias=0.5)
-        nc.scalar.activation(sq1[:], e1[:], ACT.Square, scale=ratio[:], bias=-2.0)
-        nc.scalar.activation(half_log[:], sq1[:], ACT.Identity, scale=-0.25, bias=v1[:])
+        nc.scalar.activation(exp_guess[:], bits, ACT.Exp, scale=-LOG_PER_BIT, bias=-2.0 * HALF_LOG_OFFSET)
+        nc.scalar.activation(guess[:], bits, ACT.Identity, scale=0.5 * LOG_PER_BIT, bias=HALF_LOG_OFFSET + 0.5)
+        nc.scalar.activation(square1[:], exp_guess[:], ACT.Square, scale=ratio[:], bias=-2.0)
+        nc.scalar.activation(step1[:], square1[:], ACT.Identity, scale=-0.25, bias=guess[:])
+        nc.scalar.activation(exp_step1[:], step1[:], ACT.Exp, scale=-2.0, bias=0.5)
+        nc.scalar.activation(square2[:], exp_step1[:], ACT.Square, scale=ratio[:], bias=-2.0)
+        nc.scalar.activation(half_log[:], square2[:], ACT.Identity, scale=-0.25, bias=step1[:])
         nc.scalar.activation(neg_inv_a[:], inv_a[:], ACT.Copy, scale=-1.0)
-        tilt = sbuf("tilt", [P, PACK, P])
-        share_sq = sbuf("share_sq", [P, PACK, P])
-        nc.scalar.activation(tilt[:], gap[:], ACT.Tanh, scale=-0.5, bias=half_log[:])
+        neg_tilt = sbuf("neg_tilt", [P, I])
+        nc.scalar.activation(neg_tilt[:], gap[:], ACT.Tanh, scale=-0.5, bias=half_log[:])
 
-        gather(val_words, val_word_pool)
-        nc.tensor.matmul_mx(
-            out=ta[:], lhsT=late_codes[:, 0, :].bitcast(FP8X4), lhsT_scale=late_scales[:, 0, :],
-            rhs=key_words[:].bitcast(FP8X4), rhs_scale=key_scales[:], start=True, stop=True,
-        )
-        size_turned = ps_turn.tile([P, P], F32, name="size_turned", tag="turn")
-        size_cols = sbuf("size_cols", [P, 4])
-        nc.tensor.transpose(size_turned[:], size_rows[:], identity[:])
-        nc.scalar.copy(size_cols[:], size_turned[:, 0:4])
-        c0_by_slot = ps.tile([P, 4, Q], F32, name="c0_by_slot", tag="bank_c")
-        cs_by_slot = sbuf("cs_by_slot", [P, 4, Q], tag="gap")
+        gather(val_words[:], val_word_pool)
+        ta = ps.tile([P, I], F32, name="ta", tag="bank_ta")
+        product(ta[:], late_codes[:, 0, :], late_scales[:, 0, :], key_words[:], key_scales[:])
+        slot_rows_turned = ps_turn.tile([P, P], F32, name="slot_rows_turned", tag="turn")
+        slot_cols = sbuf("slot_cols", [P, 2 * PLACES])
+        nc.tensor.transpose(slot_rows_turned[:], slot_rows[:], identity[:])
+        nc.scalar.copy(slot_cols[:], slot_rows_turned[:, 0 : 2 * PLACES])
+        c0_by_slot = ps.tile([P, I // P, Q], F32, name="c0_by_slot", tag="bank_c")
+        cs_by_slot = sbuf("cs_by_slot", [P, I // P, Q], after="gap")
         cs = ps.tile([P, I], F32, name="cs", tag="bank_cs")
-        for r in range(4):
-            cols = slice(r * P, (r + 1) * P)
-            nc.tensor.matmul_mx(
-                out=c0_by_slot[:, r, :], lhsT=val_words[:, cols].bitcast(FP8X4), lhsT_scale=val_scales[VALS_PLANE:P, cols],
-                rhs=late_codes[:, 1, :].bitcast(FP8X4), rhs_scale=late_scales[:, 1, :], start=True, stop=True,
+        share_sq = sbuf("share_sq", [P, I])
+        for r in range(I // P):
+            slots = slice(r * P, (r + 1) * P)
+            product(
+                c0_by_slot[:, r, :], val_words[:, slots], val_scales[VAL_PLANE_ROW:P, slots],
+                late_codes[:, 1, :], late_scales[:, 1, :],
             )
-        for r in range(4):
-            nc.scalar.activation(cs_by_slot[:, r, :], c0_by_slot[:, r, :], ACT.Copy, scale=size_cols[:, r : r + 1])
-        nc.scalar.activation(share_sq[:], tilt[:], ACT.Square, scale=-0.5, bias=0.5)
-        for r in range(4):
+        for r in range(I // P):
+            nc.scalar.activation(cs_by_slot[:, r, :], c0_by_slot[:, r, :], ACT.Copy, scale=slot_cols[:, r : r + 1])
+        nc.scalar.activation(share_sq[:], neg_tilt[:], ACT.Square, scale=-0.5, bias=0.5)
+        for r in range(I // P):
             nc.tensor.transpose(cs[:, r * P : (r + 1) * P], cs_by_slot[:, r, :], identity[:])
 
-        tpa = sbuf("tpa", [P, PACK, P], tag="val_word_pool")
-        sum_tpa = column("sum_tpa")
-        neg_mean = column("neg_mean")
-        nc.vector.scalar_tensor_tensor(tpa[:], dealt(ta), 1.0, pa[:], ALU.mult, ALU.mult, accum_out=sum_tpa[:])
-        nc.scalar.activation(neg_mean[:], sum_tpa[:], ACT.Copy, scale=neg_inv_a[:])
-        picked = []
+        picked = [sbuf("picked%d" % c, [P, I], BF16) for c in range(D // P)]
 
         def pick(c):
-            picked.append(sbuf("picked%d" % c, [P, I], BF16))
-            nc.vector.tensor_copy(picked[c][:], key_rows[c][:].indirect(offsets[:]))
+            gather(list_order(picked[c][:]), key_rows[c])
 
+        tpa = sbuf("tpa", [P, I], after="val_word_pool")
+        sum_tpa = column("sum_tpa")
+        neg_mean = column("neg_mean")
+        nc.vector.scalar_tensor_tensor(tpa[:], ta[:], 1.0, pa[:], ALU.mult, ALU.mult, accum_out=sum_tpa[:])
+        nc.scalar.activation(neg_mean[:], sum_tpa[:], ACT.Copy, scale=neg_inv_a[:])
         pick(0)
         pick(1)
-        ut = sbuf("ut", [P, PACK, P], tag="key_rows1")
-        nc.vector.scalar_tensor_tensor(ut[:], dealt(ta), neg_mean[:], tilt[:], ALU.add, ALU.mult)
-        pc = sbuf("pc", [P, PACK, P], tag="key_rows0")
-        nc.vector.scalar_tensor_tensor(pc[:], dealt(cs), neg_inv_a[:], pa[:], ALU.mult, ALU.mult)
-        y = sbuf("y", [P, PACK, P])
-        neg_g = column("neg_g")
-        nc.vector.scalar_tensor_tensor(y[:], pc[:], 1.0, share_sq[:], ALU.mult, ALU.mult, accum_out=neg_g[:])
-        z = sbuf("z", [P, PACK, P])
+        neg_ut = sbuf("neg_ut", [P, I], after="key_rows0")
+        nc.vector.scalar_tensor_tensor(neg_ut[:], ta[:], neg_mean[:], neg_tilt[:], ALU.add, ALU.mult)
+        cs_pa = sbuf("cs_pa", [P, I], after="key_rows1")
+        nc.vector.tensor_tensor(by_place(cs_pa[:]), dealt_order(cs[:]), by_place(pa[:]), ALU.mult)
+        neg_y = sbuf("neg_y", [P, I])
+        neg_sum_y = column("neg_sum_y")
+        nc.vector.scalar_tensor_tensor(
+            neg_y[:], cs_pa[:], neg_inv_a[:], share_sq[:], ALU.mult, ALU.mult, accum_out=neg_sum_y[:]
+        )
+        z = sbuf("z", [P, I])
         sum_z = column("sum_z")
-        nc.vector.scalar_tensor_tensor(z[:], y[:], 1.0, ut[:], ALU.mult, ALU.mult, accum_out=sum_z[:])
-
+        nc.vector.scalar_tensor_tensor(z[:], neg_y[:], 1.0, neg_ut[:], ALU.mult, ALU.mult, accum_out=sum_z[:])
         pick(2)
         pick(3)
-        alpha = column("alpha")
-        gamma = column("gamma")
-        beta = column("beta")
-        term_tpa = sbuf("term_tpa", [P, PACK, P])
-        term_pa = sbuf("term_pa", [P, PACK, P])
-        nc.scalar.activation(alpha[:], neg_g[:], ACT.Copy, scale=inv_a[:])
-        nc.scalar.activation(gamma[:], alpha[:], ACT.Copy, scale=neg_mean[:])
-        nc.scalar.activation(term_tpa[:], tpa[:], ACT.Copy, scale=alpha[:])
-        nc.scalar.activation(beta[:], sum_z[:], ACT.Identity, scale=neg_inv_a[:], bias=gamma[:])
-        nc.scalar.activation(term_pa[:], pa[:], ACT.Copy, scale=beta[:])
 
-        tda_turned = ps.tile([P, PACK, Q], F32, name="tda_turned", tag="bank_a")
-        terms = [z, term_tpa, term_pa]
+        tpa_factor = column("tpa_factor")
+        mean_part = column("mean_part")
+        pa_factor = column("pa_factor")
+        tpa_term = sbuf("tpa_term", [P, I])
+        pa_term = sbuf("pa_term", [P, I])
+        nc.scalar.activation(tpa_factor[:], neg_sum_y[:], ACT.Copy, scale=inv_a[:])
+        nc.scalar.activation(mean_part[:], tpa_factor[:], ACT.Copy, scale=neg_mean[:])
+        nc.scalar.activation(tpa_term[:], tpa[:], ACT.Copy, scale=tpa_factor[:])
+        nc.scalar.activation(pa_factor[:], sum_z[:], ACT.Identity, scale=neg_inv_a[:], bias=mean_part[:])
+        nc.scalar.activation(pa_term[:], pa[:], ACT.Copy, scale=pa_factor[:])
+        tda_turned = ps.tile([P, PLACES, Q], F32, name="tda_turned", tag="bank_a")
+        terms = [z, tpa_term, pa_term]
         for n, term in enumerate(terms):
-            for t in range(PACK):
+            for t in range(PLACES):
                 nc.tensor.matmul(
-                    tda_turned[:, t, :], lhsT=term[:, t, :], rhs=identity[:], is_transpose=True,
-                    start=(n == 0 and t == 0), stop=(n == len(terms) - 1 and t == PACK - 1),
+                    tda_turned[:, t, :], lhsT=term[:, t * P : (t + 1) * P], rhs=identity[:], is_transpose=True,
+                    start=(n == 0 and t == 0), stop=(n == len(terms) - 1 and t == PLACES - 1),
                 )
-        g_woven = sbuf("g_woven", [P, Q, PACK], BF16, tag="key_rows3")
-        g_codes = sbuf("g_codes", [P, Q], U32)
-        g_scales = sbuf("g_scales", [P, Q], U8)
+        weight_woven = sbuf("weight_woven", [P, Q, PLACES], BF16, after="key_rows3")
+        weight_codes = sbuf("weight_codes", [P, Q], U32)
+        weight_scales = sbuf("weight_scales", [P, Q], U8)
         nc.vector.tensor_tensor(
-            g_woven[:], tda_turned[:].rearrange("p t q -> p q t"),
-            fs_by_place[:].unsqueeze(1).to_broadcast([P, Q, PACK]), ALU.mult,
+            weight_woven[:], tda_turned[:].rearrange("p t q -> p q t"),
+            slot_cols[:, PLACES : 2 * PLACES].unsqueeze(1).to_broadcast([P, Q, PLACES]), ALU.mult,
         )
-        nc.vector.quantize_mx(
-            out=g_codes[:].bitcast(FP8X4), scales=g_scales[:], in_=g_woven[:].rearrange("p q t -> p (q t)")
-        )
+        quantise(weight_codes[:], weight_scales[:], weight_woven[:].rearrange("p q t -> p (q t)"))
 
-        for half, tag in enumerate(("bank_b", "bank_c")):
-            kt_woven = sbuf("kt_woven%d" % half, [P, 2, P * PACK], BF16)
-            kt_codes = sbuf("kt_codes%d" % half, [P, 2 * P], U32)
-            kt_scales = sbuf("kt_scales%d" % half, [P, 2 * P], U8)
+        width = D // 2
+        for half, bank in enumerate(("bank_b", "bank_c")):
+            kt_woven = sbuf("kt_woven%d" % half, [P, 2, P, PLACES], BF16)
+            kt_codes = sbuf("kt_codes%d" % half, [P, width], U32)
+            kt_scales = sbuf("kt_scales%d" % half, [P, width], U8)
             for n in range(2):
-                c = 2 * half + n
-                pairs = sbuf("pairs%d" % c, [P, 2, P])
-                nc.scalar.copy(pairs[:], picked[c][:].bitcast(F32).rearrange("p (s u) -> p u s", u=2))
-                turned = ps_turn.tile([P, 2, P], F32, name="turned", tag="turn")
-                for u in range(2):
-                    nc.tensor.transpose(turned[:, u, :], pairs[:, u, :], identity[:])
-                nc.scalar.copy(
-                    kt_woven[:, n, :].bitcast(F32).rearrange("p (d u) -> p d u", u=2), turned[:].rearrange("p u d -> p d u")
-                )
-            nc.vector.quantize_mx(
-                out=kt_codes[:].bitcast(FP8X4), scales=kt_scales[:], in_=kt_woven[:].rearrange("p n w -> p (n w)")
-            )
-            cols = slice(half * 2 * P, (half + 1) * 2 * P)
-            gq = ps.tile([P, 2 * P], F32, name="gq%d" % half, tag=tag)
-            nc.tensor.matmul_mx(
-                out=gq[:], lhsT=g_codes[:].bitcast(FP8X4), lhsT_scale=g_scales[:],
-                rhs=kt_codes[:].bitcast(FP8X4), rhs_scale=kt_scales[:], start=True, stop=True,
-            )
-            result = sbuf("result%d" % half, [P, 2 * P])
-            nc.vector.tensor_tensor(result[:], gq[:], residual[:, cols], ALU.add)
-            nc.sync.dma_start(out=out[:, cols], in_=result[:])
+                rows = picked[2 * half + n]
+                kt_turned = ps_turn.tile([P, PLACES, P], BF16, name="kt_turned", tag="turn")
+                for t in range(PLACES):
+                    nc.tensor.transpose(kt_turned[:, t, :], rows[:, t * P : (t + 1) * P], identity_bf[:])
+                nc.scalar.copy(kt_woven[:, n, :, :], kt_turned[:].rearrange("p t d -> p d t"))
+            quantise(kt_codes[:], kt_scales[:], kt_woven[:].rearrange("p n d t -> p (n d t)"))
+            features = slice(half * width, (half + 1) * width)
+            gq = ps.tile([P, width], F32, name="gq%d" % half, tag=bank)
+            product(gq[:], weight_codes[:], weight_scales[:], kt_codes[:], kt_scales[:])
+            result = sbuf("result%d" % half, [P, width])
+            nc.vector.tensor_tensor(result[:], gq[:], residual[:, features], ALU.add)
+            nc.sync.dma_start(out=out[:, features], in_=result[:])

import math
from contextlib import ExitStack

import concourse.mybir as mybir
from concourse.masks import make_identity

D, T, I, Q = 512, 2048, 512, 128
FLOPS = 5 * 2 * Q * I * D

F32 = mybir.dt.float32
BF16 = mybir.dt.bfloat16
I32 = mybir.dt.int32
U32 = mybir.dt.uint32
U16 = mybir.dt.uint16
U8 = mybir.dt.uint8
FP8X4 = mybir.dt.float8_e4m3fn_x4
ACT = mybir.ActivationFunctionType
ALU = mybir.AluOpType

P = 128
PLACES = 4
RUN = 8
QUADRANT = 32
VAL_PLANE_ROW = 4
LOG_PER_BIT = math.log(2.0) / 2.0**23
HALF_LOG_OFFSET = -44.0


def tile_attend_hvagreement_q_kernel(
    tc, query, query2, keys_words, keys_scales, gout, vals_words, vals_scales, size, dquery, fs, keyrows, res, offs, out
):
    nc = tc.nc
    with ExitStack() as ctx:
        sb = ctx.enter_context(tc.tile_pool(name="sb", bufs=1))
        ps = ctx.enter_context(tc.psum_pool(name="ps", bufs=1))
        ps_turn = ctx.enter_context(tc.psum_pool(name="ps_turn", bufs=3))

        def sbuf(name, shape, dtype=F32, after=None):
            return sb.tile(shape, dtype, name=name, tag=after or name, align_bytes=64)

        def column(name, after=None):
            return sbuf(name, [P, 1], after=after)

        def list_order(dealt_tile, run=RUN):
            return dealt_tile.rearrange("p (t g j) -> p g t j", t=PLACES, j=run)

        def dealt_order(listed_tile, run=RUN):
            return listed_tile.rearrange("p (g t j) -> p t g j", t=PLACES, j=run)

        def by_place(tile, run=RUN):
            return tile.rearrange("p (t g j) -> p t g j", t=PLACES, j=run)

        def product(bank, left_codes, left_scales, right_codes, right_scales):
            nc.tensor.matmul_mx(
                out=bank, lhsT=left_codes.bitcast(FP8X4), lhsT_scale=left_scales,
                rhs=right_codes.bitcast(FP8X4), rhs_scale=right_scales, start=True, stop=True,
            )

        def quantise(codes, scales, woven):
            nc.vector.quantize_mx(out=codes.bitcast(FP8X4), scales=scales, in_=woven)

        offsets = sb.tile([P, I // 16], U16, name="offsets")
        key_scale_pool = sbuf("key_scale_pool", [P, T], U8)
        val_scale_pool = sbuf("val_scale_pool", [P, T], U8)
        key_word_pool = sbuf("key_word_pool", [P, T], U32)
        val_word_pool = sbuf("val_word_pool", [P, T], U32)
        query_raw = sbuf("query_raw", [P, PLACES, Q])
        query2_raw = sbuf("query2_raw", [P, PLACES, Q])
        dquery_raw = sbuf("dquery_raw", [P, PLACES, Q])
        gout_raw = sbuf("gout_raw", [P, PLACES, Q])
        key_rows = [sbuf("key_rows%d" % c, [P, T]) for c in range(D // P)]
        slot_rows = sbuf("slot_rows", [P, P])
        residual = sbuf("residual", [P, D])
        identity = sbuf("identity", [P, P])
        identity_bf = sbuf("identity_bf", [P, P], BF16)
        zero = column("zero")
        table_warm = column("table_warm")

        nc.vector.memset(key_scale_pool[:].bitcast(I32), 0)
        nc.gpsimd.memset(val_scale_pool[:].bitcast(I32), 0)
        nc.gpsimd.memset(zero[:], 0.0)
        nc.scalar.activation(table_warm[:], zero[:], ACT.Exp)
        nc.gpsimd.memset(slot_rows[:], 0.0)
        nc.gpsimd.dma_start(out=slot_rows[0:PLACES, :], in_=size.rearrange("o (r c) -> (o r) c", r=PLACES))
        nc.gpsimd.dma_start(
            out=slot_rows[PLACES : 2 * PLACES, :].rearrange("t (g j) -> t g j", j=RUN),
            in_=fs.rearrange("o (g t j) -> (o t) g j", t=PLACES, j=RUN),
        )
        make_identity(nc, identity[:])
        make_identity(nc, identity_bf[:])

        def load_rows(raw, src):
            nc.sync.dma_start(out=raw[:], in_=src.rearrange("(p t) q -> p t q", t=PLACES))

        def load_scales(pool, src, first_row):
            for quad in range(P // QUADRANT):
                row = QUADRANT * quad + first_row
                nc.sync.dma_start(out=pool[row : row + 4, :].bitcast(I32), in_=src[0, 4 * quad : 4 * quad + 4, :].bitcast(I32))

        def load_words(pool, src):
            nc.sync.dma_start(out=pool[:].bitcast(I32), in_=src[0].rearrange("p n t -> p (n t)").bitcast(I32))

        nc.sync.dma_start(offsets[:], offs)
        load_rows(query_raw, query)
        load_scales(key_scale_pool, keys_scales, 0)
        load_words(key_word_pool, keys_words)
        load_rows(query2_raw, query2)
        load_scales(val_scale_pool, vals_scales, VAL_PLANE_ROW)
        load_rows(dquery_raw, dquery)
        load_rows(gout_raw, gout)
        load_words(val_word_pool, vals_words)
        for c in range(D // P):
            nc.sync.dma_start(out=key_rows[c][:], in_=keyrows[c * P : (c + 1) * P, :])
        nc.sync.dma_start(out=residual[:], in_=res)

        def gather(dst, pool):
            nc.vector.tensor_copy(dst, pool[:].indirect(offsets[:]))

        def weave(woven, raw):
            nc.scalar.copy(woven, raw[:].rearrange("p t q -> p q t"))

        def quantise_rows(name, raw):
            woven = sbuf(name + "_woven", [P, Q, PLACES], BF16)
            codes = sbuf(name + "_codes", [P, Q], U32)
            scales = sbuf(name + "_scales", [P, Q], U8)
            weave(woven[:], raw)
            quantise(codes[:], scales[:], woven[:].rearrange("p q t -> p (q t)"))
            return codes, scales

        listed_key_scales = sbuf("listed_key_scales", [P, I], U8)
        key_scales = sbuf("key_scales", [P, I], U8)
        key_words = sbuf("key_words", [P, I], U32)
        val_scales = sbuf("val_scales", [P, I], U8)
        val_words = sbuf("val_words", [P, I], U32)
        gather(listed_key_scales[:], key_scale_pool)
        query_codes, query_scales = quantise_rows("query", query_raw)
        nc.vector.tensor_copy(
            by_place(key_scales[:].bitcast(I32), RUN // 4), dealt_order(listed_key_scales[:].bitcast(I32), RUN // 4)
        )
        gather(list_order(key_words[:]), key_word_pool)
        query2_codes, query2_scales = quantise_rows("query2", query2_raw)
        a = ps.tile([P, I], F32, name="a", tag="bank_a")
        b = ps.tile([P, I], F32, name="b", tag="bank_b")
        product(a[:], query_codes[:], query_scales[:], key_words[:], key_scales[:])
        product(b[:], query2_codes[:], query2_scales[:], key_words[:], key_scales[:])
        gather(val_scales[:], val_scale_pool)
        late_woven = sbuf("late_woven", [P, 2, Q, PLACES], BF16)
        late_codes = sbuf("late_codes", [P, 2, Q], U32)
        late_scales = sbuf("late_scales", [P, 2, Q], U8)
        weave(late_woven[:, 0, :, :], dquery_raw)
        weave(late_woven[:, 1, :, :], gout_raw)

        neg_a = sbuf("neg_a", [P, I])
        neg_b = sbuf("neg_b", [P, I])
        neg_max_a = column("neg_max_a")
        neg_max_b = column("neg_max_b")
        nc.vector.tensor_scalar(neg_a[:], a[:], -1.0, None, ALU.mult, ALU.min, accum_out=neg_max_a[:])
        nc.vector.tensor_scalar(neg_b[:], b[:], -1.0, None, ALU.mult, ALU.min, accum_out=neg_max_b[:])
        pa = sbuf("pa", [P, I], after="gout_raw")
        sum_a = column("sum_a", after="dquery_raw")
        pb = sbuf("pb", [P, I], BF16)
        sum_b = column("sum_b")
        nc.scalar.activation(pa[:], a[:], ACT.Exp, bias=neg_max_a[:], accum_out=sum_a[:])
        nc.scalar.activation(pb[:], b[:], ACT.Exp, bias=neg_max_b[:], accum_out=sum_b[:])
        max_gap = column("max_gap")
        gap = sbuf("gap", [P, I])
        inv_a = column("inv_a")
        nc.vector.tensor_tensor(max_gap[:], neg_max_b[:], neg_max_a[:], ALU.subtract)
        nc.vector.scalar_tensor_tensor(gap[:], neg_a[:], max_gap[:], neg_b[:], ALU.add, ALU.subtract)
        nc.vector.reciprocal(inv_a[:], sum_a[:])
        quantise(
            late_codes[:].rearrange("p n q -> p (n q)"),
            late_scales[:].rearrange("p n q -> p (n q)"),
            late_woven[:].rearrange("p n q t -> p (n q t)"),
        )

        ratio = column("ratio")
        exp_guess = column("exp_guess")
        guess = column("guess")
        square1 = column("square1")
        step1 = column("step1")
        exp_step1 = column("exp_step1")
        square2 = column("square2")
        half_log = column("half_log")
        neg_inv_a = column("neg_inv_a")
        nc.scalar.activation(ratio[:], sum_b[:], ACT.Copy, scale=inv_a[:])
        bits = ratio[:].bitcast(U32)
        nc.scalar.activation(exp_guess[:], bits, ACT.Exp, scale=-LOG_PER_BIT, bias=-2.0 * HALF_LOG_OFFSET)
        nc.scalar.activation(guess[:], bits, ACT.Identity, scale=0.5 * LOG_PER_BIT, bias=HALF_LOG_OFFSET + 0.5)
        nc.scalar.activation(square1[:], exp_guess[:], ACT.Square, scale=ratio[:], bias=-2.0)
        nc.scalar.activation(step1[:], square1[:], ACT.Identity, scale=-0.25, bias=guess[:])
        nc.scalar.activation(exp_step1[:], step1[:], ACT.Exp, scale=-2.0, bias=0.5)
        nc.scalar.activation(square2[:], exp_step1[:], ACT.Square, scale=ratio[:], bias=-2.0)
        nc.scalar.activation(half_log[:], square2[:], ACT.Identity, scale=-0.25, bias=step1[:])
        nc.scalar.activation(neg_inv_a[:], inv_a[:], ACT.Copy, scale=-1.0)
        neg_tilt = sbuf("neg_tilt", [P, I])
        nc.scalar.activation(neg_tilt[:], gap[:], ACT.Tanh, scale=-0.5, bias=half_log[:])

        gather(val_words[:], val_word_pool)
        ta = ps.tile([P, I], F32, name="ta", tag="bank_ta")
        product(ta[:], late_codes[:, 0, :], late_scales[:, 0, :], key_words[:], key_scales[:])
        slot_rows_turned = ps_turn.tile([P, P], F32, name="slot_rows_turned", tag="turn")
        slot_cols = sbuf("slot_cols", [P, 2 * PLACES])
        nc.tensor.transpose(slot_rows_turned[:], slot_rows[:], identity[:])
        nc.scalar.copy(slot_cols[:], slot_rows_turned[:, 0 : 2 * PLACES])
        c0_by_slot = ps.tile([P, I // P, Q], F32, name="c0_by_slot", tag="bank_c")
        cs_by_slot = sbuf("cs_by_slot", [P, I // P, Q], after="gap")
        cs = ps.tile([P, I], F32, name="cs", tag="bank_cs")
        share_sq = sbuf("share_sq", [P, I])
        for r in range(I // P):
            slots = slice(r * P, (r + 1) * P)
            product(
                c0_by_slot[:, r, :], val_words[:, slots], val_scales[VAL_PLANE_ROW:P, slots],
                late_codes[:, 1, :], late_scales[:, 1, :],
            )
        for r in range(I // P):
            nc.scalar.activation(cs_by_slot[:, r, :], c0_by_slot[:, r, :], ACT.Copy, scale=slot_cols[:, r : r + 1])
        nc.scalar.activation(share_sq[:], neg_tilt[:], ACT.Square, scale=-0.5, bias=0.5)
        for r in range(I // P):
            nc.tensor.transpose(cs[:, r * P : (r + 1) * P], cs_by_slot[:, r, :], identity[:])

        picked = [sbuf("picked%d" % c, [P, I], BF16) for c in range(D // P)]

        def pick(c):
            gather(list_order(picked[c][:]), key_rows[c])

        tpa = sbuf("tpa", [P, I], after="val_word_pool")
        sum_tpa = column("sum_tpa")
        neg_mean = column("neg_mean")
        nc.vector.scalar_tensor_tensor(tpa[:], ta[:], 1.0, pa[:], ALU.mult, ALU.mult, accum_out=sum_tpa[:])
        nc.scalar.activation(neg_mean[:], sum_tpa[:], ACT.Copy, scale=neg_inv_a[:])
        pick(0)
        pick(1)
        neg_ut = sbuf("neg_ut", [P, I], after="key_rows0")
        nc.vector.scalar_tensor_tensor(neg_ut[:], ta[:], neg_mean[:], neg_tilt[:], ALU.add, ALU.mult)
        cs_pa = sbuf("cs_pa", [P, I], after="key_rows1")
        nc.vector.tensor_tensor(by_place(cs_pa[:]), dealt_order(cs[:]), by_place(pa[:]), ALU.mult)
        neg_y = sbuf("neg_y", [P, I])
        neg_sum_y = column("neg_sum_y")
        nc.vector.scalar_tensor_tensor(
            neg_y[:], cs_pa[:], neg_inv_a[:], share_sq[:], ALU.mult, ALU.mult, accum_out=neg_sum_y[:]
        )
        z = sbuf("z", [P, I])
        sum_z = column("sum_z")
        nc.vector.scalar_tensor_tensor(z[:], neg_y[:], 1.0, neg_ut[:], ALU.mult, ALU.mult, accum_out=sum_z[:])
        pick(2)
        pick(3)

        tpa_factor = column("tpa_factor")
        mean_part = column("mean_part")
        pa_factor = column("pa_factor")
        tpa_term = sbuf("tpa_term", [P, I])
        pa_term = sbuf("pa_term", [P, I])
        nc.scalar.activation(tpa_factor[:], neg_sum_y[:], ACT.Copy, scale=inv_a[:])
        nc.scalar.activation(mean_part[:], tpa_factor[:], ACT.Copy, scale=neg_mean[:])
        nc.scalar.activation(tpa_term[:], tpa[:], ACT.Copy, scale=tpa_factor[:])
        nc.scalar.activation(pa_factor[:], sum_z[:], ACT.Identity, scale=neg_inv_a[:], bias=mean_part[:])
        nc.scalar.activation(pa_term[:], pa[:], ACT.Copy, scale=pa_factor[:])
        tda_turned = ps.tile([P, PLACES, Q], F32, name="tda_turned", tag="bank_a")
        terms = [z, tpa_term, pa_term]
        for n, term in enumerate(terms):
            for t in range(PLACES):
                nc.tensor.matmul(
                    tda_turned[:, t, :], lhsT=term[:, t * P : (t + 1) * P], rhs=identity[:], is_transpose=True,
                    start=(n == 0 and t == 0), stop=(n == len(terms) - 1 and t == PLACES - 1),
                )
        weight_woven = sbuf("weight_woven", [P, Q, PLACES], BF16, after="key_rows3")
        weight_codes = sbuf("weight_codes", [P, Q], U32)
        weight_scales = sbuf("weight_scales", [P, Q], U8)
        nc.vector.tensor_tensor(
            weight_woven[:], tda_turned[:].rearrange("p t q -> p q t"),
            slot_cols[:, PLACES : 2 * PLACES].unsqueeze(1).to_broadcast([P, Q, PLACES]), ALU.mult,
        )
        quantise(weight_codes[:], weight_scales[:], weight_woven[:].rearrange("p q t -> p (q t)"))

        width = D // 2
        for half, bank in enumerate(("bank_b", "bank_c")):
            kt_woven = sbuf("kt_woven%d" % half, [P, 2, P, PLACES], BF16)
            kt_codes = sbuf("kt_codes%d" % half, [P, width], U32)
            kt_scales = sbuf("kt_scales%d" % half, [P, width], U8)
            for n in range(2):
                rows = picked[2 * half + n]
                kt_turned = ps_turn.tile([P, PLACES, P], BF16, name="kt_turned", tag="turn")
                for t in range(PLACES):
                    nc.tensor.transpose(kt_turned[:, t, :], rows[:, t * P : (t + 1) * P], identity_bf[:])
                nc.scalar.copy(kt_woven[:, n, :, :], kt_turned[:].rearrange("p t d -> p d t"))
            quantise(kt_codes[:], kt_scales[:], kt_woven[:].rearrange("p n d t -> p (n d t)"))
            features = slice(half * width, (half + 1) * width)
            gq = ps.tile([P, width], F32, name="gq%d" % half, tag=bank)
            product(gq[:], weight_codes[:], weight_scales[:], kt_codes[:], kt_scales[:])
            result = sbuf("result%d" % half, [P, width])
            nc.vector.tensor_tensor(result[:], gq[:], residual[:, features], ALU.add)
            nc.sync.dma_start(out=out[:, features], in_=result[:])
